import numpy as np
import ml_dtypes


def mxq(x, axis, fmt="e4m3"):
    dtype, down = {"e4m3": (ml_dtypes.float8_e4m3fn, 7), "e5m2": (ml_dtypes.float8_e5m2, 14)}[fmt]
    v = np.moveaxis(np.asarray(x, np.float32).astype(ml_dtypes.bfloat16).astype(np.float64), axis, -1)
    blocks = v.reshape(v.shape[:-1] + (-1, 32))
    amax = np.abs(blocks).max(-1, keepdims=True)
    byte = np.maximum(np.where(amax > 0, np.frexp(amax)[1] - 1 + 127, 0) - down, 1)
    scale = np.exp2(byte - 127.0)
    codes = (blocks / scale).astype(np.float32).astype(dtype).astype(np.float64)
    return np.moveaxis((codes * scale).reshape(v.shape), -1, axis)


WIDE = False


def mx_kscale(k):
    if not WIDE:
        return np.ones(k)
    levels = np.array([10, -10, 5, -5, 0])
    if k % 512:
        return np.exp2(np.random.permutation(np.resize(levels, k // 32))).repeat(32)
    a = np.empty((k // 512, 16))
    for p in range(k // 512):
        a[p, :8] = np.random.permutation(np.resize(levels, 8))
        for g in range(8):
            far = levels[np.abs(levels - a[p, g]) >= 10]
            a[p, g + 8] = far[np.random.randint(len(far))]
    return np.exp2(a.ravel()).repeat(32)


def f64(x):
    return np.asarray(x).astype(np.float64)


def striped(idx):
    return np.tile(idx.reshape(-1, 16).T, (8, 1)).astype(np.uint16)


def unstriped(offs):
    return offs[:16].T.reshape(-1).astype(np.int64)


def pack_weight(w):
    k, n = w.shape
    w = f64(np.asarray(w, np.float32).astype(ml_dtypes.bfloat16)).reshape(k // 32, 32, n)
    amax = np.abs(w).max(1)
    byte = np.clip(np.where(amax > 0, np.frexp(amax)[1] - 1 + 127 - 7, 1), 1, 254)
    scaled = (w * np.exp2(127.0 - byte)[:, None, :]).reshape(k, n).astype(np.float32)
    words = np.ascontiguousarray(scaled.reshape(k // 512, 128, 4, n).transpose(0, 1, 3, 2)).astype(ml_dtypes.float8_e4m3fn).view(np.uint8)
    return words, np.ascontiguousarray(byte.astype(np.uint8).reshape(k // 512, 16, n))


def unpack_weight(words, scales):
    g, p, n, _ = words.shape
    vals = np.ascontiguousarray(words).view(ml_dtypes.float8_e4m3fn).astype(np.float64) * np.repeat(np.exp2(scales.astype(np.float64) - 127.0), 8, axis=1)[..., None]
    return vals.transpose(0, 1, 3, 2).reshape(g * 512, n)


def relu(v):
    return np.maximum(v, 0.0)


K, T, S, D, N, H = 512, 2048, 512, 4, 128, 512


def setup_inputs():
    n = np.random.standard_normal
    s = mx_kscale(K)[:, None]
    u = mx_kscale(H)
    packed_xT = pack_weight(n((K, T)) * s)
    return {
        "x_words": packed_xT[0],
        "x_scales": packed_xT[1],
        "w1": (n((K, H)) / np.sqrt(K) / s).astype(np.float32),
        "noise": (np.random.uniform(0.3, 1.0, (H, S))).astype(np.float32),
        "unit": (np.random.uniform(0.6, 1.4, (H, 1)) * u[:, None]).astype(np.float32),
        "w2": (n((H, N)) / np.sqrt(H) / u[:, None]).astype(np.float32),
        "offs": striped(np.random.permutation(T)[:S]),
        "itf": striped(np.random.permutation(S)),
    }


def reference(x_words, x_scales, w1, noise, unit, w2, offs, itf):
    xq = unpack_weight(x_words, x_scales)[:, unstriped(offs)]
    y = mxq(f64(w1), 0, "e4m3").T @ xq
    gain = np.log(np.exp(y) + 1.0) + 0.2
    inv = f64(noise) / gain
    lvl = 0.25 * (inv.reshape(len(inv), -1, D).sum(axis=2) + 2.0)
    pw1 = relu(np.repeat(lvl, D, axis=1) - inv)
    exc = -1.0 * (pw1.reshape(len(pw1), -1, D).sum(axis=2)) + 2.0
    pw2 = relu(pw1 + 0.25 * np.repeat(exc, D, axis=1))
    rate = np.log(pw2 / inv + 1.0)
    hid = f64(unit) * (rate - (0.5 * pw2[:, unstriped(itf)]))
    return mxq(f64(w2), 0, "e4m3").T @ mxq(hid, 0, "e4m3")

@@ -1,0 +1,201 @@
+from contextlib import ExitStack
+
+import concourse.mybir as mybir
+
+K, T, S, D, N, H = 512, 2048, 512, 4, 128, 512
+FLOPS = 2 * K * H * S + 2 * H * N * S
+
+F32 = mybir.dt.float32
+BF16 = mybir.dt.bfloat16
+I32 = mybir.dt.int32
+U32 = mybir.dt.uint32
+U16 = mybir.dt.uint16
+U8 = mybir.dt.uint8
+FP8X4 = mybir.dt.float8_e4m3fn_x4
+ALU = mybir.AluOpType
+ACT = mybir.ActivationFunctionType
+
+P = 128
+PACK = 4
+V = S // D
+HALF = S // 2
+EXP_CAP = 1.0e13
+W1_VECTOR_SHARE = 88
+
+
+def tile_picked_ywater_rate_p_kernel(tc, x_words, x_scales, w1, noise, unit, w2, offs, itf, out):
+    nc = tc.nc
+    with ExitStack() as ctx:
+        keep = ctx.enter_context(tc.tile_pool(name="keep", bufs=1))
+        psum = ctx.enter_context(tc.psum_pool(name="psum", bufs=1))
+
+        def rows(name, dtype=F32, width=S):
+            return [keep.tile([P, width], dtype, name="%s%d" % (name, t), align_bytes=64) for t in range(PACK)]
+
+        offs_sb = keep.tile([P, S // 16], U16, name="offs_sb")
+        itf_sb = keep.tile([P, S // 16], U16, name="itf_sb")
+        x_bytes = keep.tile([P, T], U8, name="x_bytes", align_bytes=64)
+        x_codes = keep.tile([P, T], I32, name="x_codes", align_bytes=64)
+        w1_raw = keep.tile([P, PACK, H], F32, name="w1_raw", align_bytes=64)
+        w2_raw = keep.tile([P, PACK, N], F32, name="w2_raw", align_bytes=64)
+        unit_sb = keep.tile([P, PACK], F32, name="unit_sb")
+        noise_sb = keep.tile([P, PACK, S], F32, name="noise_sb", align_bytes=64)
+
+        nc.gpsimd.memset(x_bytes[:].bitcast(I32), 0)
+        nc.sync.dma_start(offs_sb[:], offs)
+        nc.sync.dma_start(out=w1_raw[:], in_=w1.rearrange("(p j) c -> p j c", j=PACK))
+        for q in range(4):
+            nc.sync.dma_start(out=x_bytes[32 * q : 32 * q + 4, :].bitcast(I32), in_=x_scales[0, 4 * q : 4 * q + 4, :].bitcast(I32))
+        nc.sync.dma_start(out=x_codes[:], in_=x_words[0].rearrange("p n t -> p (n t)").bitcast(I32))
+        nc.sync.dma_start(itf_sb[:], itf)
+        nc.sync.dma_start(out=noise_sb[:], in_=noise.rearrange("(p t) j -> p t j", t=PACK))
+        nc.sync.dma_start(out=unit_sb[:], in_=unit.rearrange("(p t) o -> p (t o)", t=PACK))
+        nc.sync.dma_start(out=w2_raw[:], in_=w2.rearrange("(p j) m -> p j m", j=PACK))
+
+        picked_bytes = keep.tile([P, S], U8, name="picked_bytes", align_bytes=64)
+        picked_codes = [keep.tile([P, HALF], U32, name="picked_codes%d" % c, align_bytes=64) for c in range(2)]
+        nc.vector.tensor_copy(picked_bytes[:], x_bytes[:].indirect(offs_sb[:]))
+
+        w1_bf = keep.tile([P, PACK, P, PACK], BF16, name="w1_bf", align_bytes=64)
+        w1_dst = w1_bf[:].rearrange("p t m j -> p m j t")
+        w1_src = w1_raw[:].rearrange("p j (m t) -> p m j t", t=PACK)
+        nc.vector.tensor_copy(out=w1_dst[:, :W1_VECTOR_SHARE], in_=w1_src[:, :W1_VECTOR_SHARE])
+        nc.scalar.copy(out=w1_dst[:, W1_VECTOR_SHARE:], in_=w1_src[:, W1_VECTOR_SHARE:])
+        w1_codes = keep.tile([P, H], U32, name="w1_codes", align_bytes=64)
+        w1_scales = keep.tile([P, H], U8, name="w1_scales", align_bytes=64)
+        nc.vector.quantize_mx(out=w1_codes[:].bitcast(FP8X4), scales=w1_scales[:], in_=w1_bf[:].rearrange("p t m j -> p (t m j)"))
+
+        y = [psum.tile([P, S], F32, name="y%d" % t) for t in range(PACK)]
+        exp_y = rows("exp_y")
+        soft = rows("soft")
+        log_inv = rows("log_inv")
+        inv = rows("inv")
+        for c in range(2):
+            half = slice(c * HALF, (c + 1) * HALF)
+            nc.vector.tensor_copy(picked_codes[c][:], x_codes[:].bitcast(U32).indirect(offs_sb[:, c * 16 : (c + 1) * 16]))
+            for t in range(PACK):
+                cols = slice(t * P, (t + 1) * P)
+                nc.tensor.matmul_mx(out=y[c * 2 + t // 2][:, (t % 2) * HALF : (t % 2 + 1) * HALF], lhsT=w1_codes[:, cols].bitcast(FP8X4), lhsT_scale=w1_scales[:, cols],
+                                    rhs=picked_codes[c][:].bitcast(FP8X4), rhs_scale=picked_bytes[:, half], start=True, stop=True)
+
+        def product(t, c):
+            return y[c * 2 + t // 2][:, (t % 2) * HALF : (t % 2 + 1) * HALF]
+
+        for c in range(2):
+            half = slice(c * HALF, (c + 1) * HALF)
+            for t in range(PACK):
+                nc.scalar.activation(out=exp_y[t][:, half], in_=product(t, c), func=ACT.Exp)
+        for t in range(PACK):
+            nc.vector.tensor_scalar(out=exp_y[t][:], in0=exp_y[t][:], scalar1=EXP_CAP, scalar2=None, op0=ALU.min)
+
+        size = keep.tile([P, PACK], F32, name="size")
+        sign = keep.tile([P, PACK], F32, name="sign")
+        half_size = keep.tile([P, PACK], F32, name="half_size")
+        quarter_size = keep.tile([P, PACK], F32, name="quarter_size")
+        nc.scalar.activation(out=size[:], in_=unit_sb[:], func=ACT.Abs)
+        nc.scalar.activation(out=half_size[:], in_=unit_sb[:], func=ACT.Abs, scale=0.5)
+        nc.scalar.activation(out=quarter_size[:], in_=unit_sb[:], func=ACT.Abs, scale=0.25)
+        nc.scalar.activation(out=sign[:], in_=unit_sb[:], func=ACT.Sign)
+
+        w2_bf = keep.tile([P, N, PACK], BF16, name="w2_bf", align_bytes=64)
+        nc.vector.tensor_tensor(out=w2_bf[:], in0=w2_raw[:].rearrange("p j m -> p m j"),
+                                in1=sign[:].unsqueeze(1).to_broadcast([P, N, PACK]), op=ALU.mult)
+        w2_codes = keep.tile([P, N], U32, name="w2_codes", align_bytes=64)
+        w2_scales = keep.tile([P, N], U8, name="w2_scales", align_bytes=64)
+        nc.vector.quantize_mx(out=w2_codes[:].bitcast(FP8X4), scales=w2_scales[:], in_=w2_bf[:].rearrange("p m j -> p (m j)"))
+
+        log_noise = exp_y
+        pair = rows("pair", width=2 * V)
+        level4 = rows("level4", width=V)
+        above4 = rows("above4")
+        pair_above = rows("pair_above", width=2 * V)
+        part = rows("part", width=V)
+        level2 = rows("level2", width=V)
+        level_scaled = rows("level_scaled", width=V)
+        log_level = rows("log_level", width=V)
+        gap = rows("gap")
+        log_ratio = rows("log_ratio")
+        fetched = rows("fetched")
+        hid = keep.tile([P, PACK, S], F32, name="hid", align_bytes=64)
+
+        def groups(tile):
+            return tile[:].rearrange("p (v d) -> p v d", d=D)
+
+        def pairs(tile):
+            return tile[:].rearrange("p (v e) -> p v e", e=2)
+
+        def spread(tile):
+            return tile[:].unsqueeze(2).to_broadcast([P, V, D])
+
+        def logs(planes):
+            for t in planes:
+                nc.scalar.activation(out=soft[t][:], in_=exp_y[t][:], func=ACT.Ln, bias=1.0)
+                for c in range(2):
+                    half = slice(c * HALF, (c + 1) * HALF)
+                    nc.vector.tensor_tensor(out=soft[t][:, half], in0=product(t, c), in1=soft[t][:, half], op=ALU.max)
+            for t in planes:
+                nc.scalar.activation(out=log_noise[t][:], in_=noise_sb[:, t, :], func=ACT.Ln)
+            for t in planes:
+                nc.scalar.activation(out=soft[t][:], in_=soft[t][:], func=ACT.Ln, bias=0.2)
+                nc.vector.tensor_tensor(out=log_inv[t][:], in0=log_noise[t][:], in1=soft[t][:], op=ALU.subtract)
+
+        def exps(planes):
+            for t in planes:
+                nc.scalar.activation(out=inv[t][:], in_=log_inv[t][:], func=ACT.Exp)
+
+        def levels(planes):
+            for t in planes:
+                nc.vector.tensor_tensor(out=pairs(pair[t]), in0=groups(inv[t])[:, :, 0:2], in1=groups(inv[t])[:, :, 2:4], op=ALU.add)
+                nc.vector.scalar_tensor_tensor(out=level4[t][:], in0=pairs(pair[t])[:, :, 0], scalar=2.0, in1=pairs(pair[t])[:, :, 1], op0=ALU.add, op1=ALU.add)
+                nc.vector.scalar_tensor_tensor(out=groups(above4[t]), in0=groups(inv[t]), scalar=4.0, in1=spread(level4[t]), op0=ALU.mult, op1=ALU.max)
+                nc.vector.tensor_tensor(out=pairs(pair_above[t]), in0=groups(above4[t])[:, :, 0:2], in1=groups(above4[t])[:, :, 2:4], op=ALU.add)
+                nc.vector.scalar_tensor_tensor(out=part[t][:], in0=pairs(pair_above[t])[:, :, 0], scalar=-0.125, in1=level4[t][:], op0=ALU.mult, op1=ALU.add)
+                nc.vector.scalar_tensor_tensor(out=level2[t][:], in0=pairs(pair_above[t])[:, :, 1], scalar=-0.125, in1=part[t][:], op0=ALU.mult, op1=ALU.add)
+                nc.scalar.activation(out=log_level[t][:], in_=level2[t][:], func=ACT.Ln, scale=0.5)
+
+        def finish(planes):
+            for t in planes:
+                nc.scalar.activation(out=level_scaled[t][:], in_=level2[t][:], func=ACT.Copy, scale=quarter_size[:, t : t + 1])
+                nc.vector.scalar_tensor_tensor(out=groups(gap[t]), in0=groups(inv[t]), scalar=half_size[:, t : t + 1], in1=spread(level_scaled[t]), op0=ALU.mult, op1=ALU.subtract)
+                for c in range(2):
+                    half = slice(c * HALF, (c + 1) * HALF)
+                    nc.scalar.activation(out=fetched[t][:, half], in_=gap[t][:].indirect(itf_sb[:, c * 16 : (c + 1) * 16]), func=ACT.Copy)
+
+        def rates(planes):
+            for t in planes:
+                nc.vector.tensor_tensor(out=groups(log_ratio[t]), in0=spread(log_level[t]), in1=groups(log_inv[t]), op=ALU.subtract)
+                nc.scalar.activation(out=log_ratio[t][:], in_=log_ratio[t][:], func=ACT.Relu, scale=size[:, t : t + 1])
+
+        def combine(planes):
+            for t in planes:
+                for c in range(2):
+                    half = slice(c * HALF, (c + 1) * HALF)
+                    nc.vector.scalar_tensor_tensor(out=hid[:, t, half], in0=fetched[t][:, half], scalar=0.0, in1=log_ratio[t][:, half], op0=ALU.min, op1=ALU.add)
+
+        every = range(PACK)
+        logs(every)
+        exps(every)
+        for t in every:
+            levels([t])
+            finish([t])
+        rates(every)
+        combine(every)
+
+        Q = 128
+        for c in range(S // Q):
+            hid_bf = keep.tile([P, Q, PACK], BF16, name="hid_bf%d" % c, align_bytes=64)
+            dst = hid_bf[:].rearrange("p (c i) t -> p c t i", i=4)
+            src = hid[:, :, c * Q : (c + 1) * Q].rearrange("p t (c i) -> p c t i", i=4)
+            if c == 1:
+                nc.scalar.copy(out=dst, in_=src)
+            else:
+                nc.vector.tensor_copy(out=dst, in_=src)
+            hid_codes = keep.tile([P, Q], U32, name="hid_codes%d" % c, align_bytes=64)
+            hid_scales = keep.tile([P, Q], U8, name="hid_scales%d" % c, align_bytes=64)
+            nc.vector.quantize_mx(out=hid_codes[:].bitcast(FP8X4), scales=hid_scales[:], in_=hid_bf[:].rearrange("p j t -> p (j t)"))
+            acc = psum.tile([P, Q], F32, name="acc%d" % c)
+            nc.tensor.matmul_mx(out=acc[:], lhsT=w2_codes[:].bitcast(FP8X4), lhsT_scale=w2_scales[:],
+                                rhs=hid_codes[:].bitcast(FP8X4), rhs_scale=hid_scales[:], start=True, stop=True)
+            res = keep.tile([P, Q], F32, name="res%d" % c, align_bytes=64)
+            nc.scalar.copy(out=res[:], in_=acc[:])
+            nc.sync.dma_start(out=out[:, c * Q : (c + 1) * Q], in_=res[:])

@@ -1,3 +1,4 @@
+import math
 from contextlib import ExitStack
 
 import concourse.mybir as mybir
@@ -20,7 +21,8 @@ PACK = 4
 V = S // D
 HALF = S // 2
 EXP_CAP = 1.0e13
-W1_VECTOR_SHARE = 88
+W1_VECTOR_SHARE = 40
+GAIN_FLOOR = 0.2
 
 
 def tile_picked_ywater_rate_p_kernel(tc, x_words, x_scales, w1, noise, unit, w2, offs, itf, out):
@@ -36,16 +38,18 @@ def tile_picked_ywater_rate_p_kernel(tc, x_words, x_scales, w1, noise, unit, w2,
         itf_sb = keep.tile([P, S // 16], U16, name="itf_sb")
         x_bytes = keep.tile([P, T], U8, name="x_bytes", align_bytes=64)
         x_codes = keep.tile([P, T], I32, name="x_codes", align_bytes=64)
-        w1_raw = keep.tile([P, PACK, H], F32, name="w1_raw", align_bytes=64)
+        w1_raw = [keep.tile([P, PACK, H // 2], F32, name="w1_raw%d" % c, align_bytes=64) for c in range(2)]
         w2_raw = keep.tile([P, PACK, N], F32, name="w2_raw", align_bytes=64)
         unit_sb = keep.tile([P, PACK], F32, name="unit_sb")
         noise_sb = keep.tile([P, PACK, S], F32, name="noise_sb", align_bytes=64)
 
         nc.gpsimd.memset(x_bytes[:].bitcast(I32), 0)
         nc.sync.dma_start(offs_sb[:], offs)
-        nc.sync.dma_start(out=w1_raw[:], in_=w1.rearrange("(p j) c -> p j c", j=PACK))
+        w1_rows = w1.rearrange("(p j) c -> p j c", j=PACK)
+        nc.sync.dma_start(out=w1_raw[0][:], in_=w1_rows[:, :, : H // 2])
         for q in range(4):
             nc.sync.dma_start(out=x_bytes[32 * q : 32 * q + 4, :].bitcast(I32), in_=x_scales[0, 4 * q : 4 * q + 4, :].bitcast(I32))
+        nc.sync.dma_start(out=w1_raw[1][:], in_=w1_rows[:, :, H // 2 :])
         nc.sync.dma_start(out=x_codes[:], in_=x_words[0].rearrange("p n t -> p (n t)").bitcast(I32))
         nc.sync.dma_start(itf_sb[:], itf)
         nc.sync.dma_start(out=noise_sb[:], in_=noise.rearrange("(p t) j -> p t j", t=PACK))
@@ -58,9 +62,11 @@ def tile_picked_ywater_rate_p_kernel(tc, x_words, x_scales, w1, noise, unit, w2,
 
         w1_bf = keep.tile([P, PACK, P, PACK], BF16, name="w1_bf", align_bytes=64)
         w1_dst = w1_bf[:].rearrange("p t m j -> p m j t")
-        w1_src = w1_raw[:].rearrange("p j (m t) -> p m j t", t=PACK)
-        nc.vector.tensor_copy(out=w1_dst[:, :W1_VECTOR_SHARE], in_=w1_src[:, :W1_VECTOR_SHARE])
-        nc.scalar.copy(out=w1_dst[:, W1_VECTOR_SHARE:], in_=w1_src[:, W1_VECTOR_SHARE:])
+        w1_src = [w1_raw[c][:].rearrange("p j (m t) -> p m j t", t=PACK) for c in range(2)]
+        split = P // 2 + W1_VECTOR_SHARE
+        nc.scalar.copy(out=w1_dst[:, : P // 2], in_=w1_src[0])
+        nc.vector.tensor_copy(out=w1_dst[:, P // 2 : split], in_=w1_src[1][:, :W1_VECTOR_SHARE])
+        nc.scalar.copy(out=w1_dst[:, split:], in_=w1_src[1][:, W1_VECTOR_SHARE:])
         w1_codes = keep.tile([P, H], U32, name="w1_codes", align_bytes=64)
         w1_scales = keep.tile([P, H], U8, name="w1_scales", align_bytes=64)
         nc.vector.quantize_mx(out=w1_codes[:].bitcast(FP8X4), scales=w1_scales[:], in_=w1_bf[:].rearrange("p t m j -> p (t m j)"))
@@ -95,6 +101,8 @@ def tile_picked_ywater_rate_p_kernel(tc, x_words, x_scales, w1, noise, unit, w2,
         nc.scalar.activation(out=size[:], in_=unit_sb[:], func=ACT.Abs)
         nc.scalar.activation(out=half_size[:], in_=unit_sb[:], func=ACT.Abs, scale=0.5)
         nc.scalar.activation(out=quarter_size[:], in_=unit_sb[:], func=ACT.Abs, scale=0.25)
+        minus_size = keep.tile([P, PACK], F32, name="minus_size")
+        nc.scalar.activation(out=minus_size[:], in_=size[:], func=ACT.Copy, scale=-1.0)
         nc.scalar.activation(out=sign[:], in_=unit_sb[:], func=ACT.Sign)
 
         w2_bf = keep.tile([P, N, PACK], BF16, name="w2_bf", align_bytes=64)
@@ -104,7 +112,8 @@ def tile_picked_ywater_rate_p_kernel(tc, x_words, x_scales, w1, noise, unit, w2,
         w2_scales = keep.tile([P, N], U8, name="w2_scales", align_bytes=64)
         nc.vector.quantize_mx(out=w2_codes[:].bitcast(FP8X4), scales=w2_scales[:], in_=w2_bf[:].rearrange("p m j -> p (m j)"))
 
-        log_noise = exp_y
+        squared = exp_y
+        recip = rows("recip")
         pair = rows("pair", width=2 * V)
         level4 = rows("level4", width=V)
         above4 = rows("above4")
@@ -127,21 +136,23 @@ def tile_picked_ywater_rate_p_kernel(tc, x_words, x_scales, w1, noise, unit, w2,
         def spread(tile):
             return tile[:].unsqueeze(2).to_broadcast([P, V, D])
 
-        def logs(planes):
-            for t in planes:
-                nc.scalar.activation(out=soft[t][:], in_=exp_y[t][:], func=ACT.Ln, bias=1.0)
-                for c in range(2):
-                    half = slice(c * HALF, (c + 1) * HALF)
-                    nc.vector.tensor_tensor(out=soft[t][:, half], in0=product(t, c), in1=soft[t][:, half], op=ALU.max)
-            for t in planes:
-                nc.scalar.activation(out=log_noise[t][:], in_=noise_sb[:, t, :], func=ACT.Ln)
-            for t in planes:
-                nc.scalar.activation(out=soft[t][:], in_=soft[t][:], func=ACT.Ln, bias=0.2)
-                nc.vector.tensor_tensor(out=log_inv[t][:], in0=log_noise[t][:], in1=soft[t][:], op=ALU.subtract)
-
-        def exps(planes):
-            for t in planes:
-                nc.scalar.activation(out=inv[t][:], in_=log_inv[t][:], func=ACT.Exp)
+        halves = [slice(c * HALF, (c + 1) * HALF) for c in range(2)]
+        lift = math.exp(GAIN_FLOOR)
+        for t in range(PACK):
+            nc.scalar.activation(out=soft[t][:], in_=exp_y[t][:], func=ACT.Ln, scale=lift, bias=lift)
+            for c, half in enumerate(halves):
+                nc.vector.scalar_tensor_tensor(out=soft[t][:, half], in0=product(t, c), scalar=GAIN_FLOOR, in1=soft[t][:, half], op0=ALU.add, op1=ALU.max)
+                if t < 2:
+                    nc.vector.tensor_tensor(out=squared[t][:, half], in0=soft[t][:, half], in1=soft[t][:, half], op=ALU.mult)
+        for half in halves:
+            nc.scalar.activation(out=recip[0][:, half], in_=squared[0][:, half], func=ACT.Abs_reciprocal_sqrt)
+        for t in range(1, PACK):
+            if t >= 2:
+                nc.scalar.activation(out=squared[t][:], in_=soft[t][:], func=ACT.Square)
+            nc.scalar.activation(out=recip[t][:], in_=squared[t][:], func=ACT.Abs_reciprocal_sqrt)
+        for t in range(PACK):
+            nc.vector.tensor_tensor(out=inv[t][:], in0=recip[t][:], in1=noise_sb[:, t, :], op=ALU.mult)
+            nc.scalar.activation(out=log_inv[t][:], in_=inv[t][:], func=ACT.Ln)
 
         def levels(planes):
             for t in planes:
@@ -153,28 +164,37 @@ def tile_picked_ywater_rate_p_kernel(tc, x_words, x_scales, w1, noise, unit, w2,
                 nc.vector.scalar_tensor_tensor(out=level2[t][:], in0=pairs(pair_above[t])[:, :, 1], scalar=-0.125, in1=part[t][:], op0=ALU.mult, op1=ALU.add)
                 nc.scalar.activation(out=log_level[t][:], in_=level2[t][:], func=ACT.Ln, scale=0.5)
 
+        LAST = PACK - 1
+
         def finish(planes):
             for t in planes:
-                nc.scalar.activation(out=level_scaled[t][:], in_=level2[t][:], func=ACT.Copy, scale=quarter_size[:, t : t + 1])
-                nc.vector.scalar_tensor_tensor(out=groups(gap[t]), in0=groups(inv[t]), scalar=half_size[:, t : t + 1], in1=spread(level_scaled[t]), op0=ALU.mult, op1=ALU.subtract)
-                for c in range(2):
-                    half = slice(c * HALF, (c + 1) * HALF)
+                if t == LAST:
+                    nc.vector.scalar_tensor_tensor(out=groups(gap[t]), in0=groups(inv[t]), scalar=2.0, in1=spread(level2[t]), op0=ALU.mult, op1=ALU.subtract)
+                    nc.vector.tensor_scalar(out=gap[t][:], in0=gap[t][:], scalar1=0.0, scalar2=quarter_size[:, t : t + 1], op0=ALU.min, op1=ALU.mult)
+                else:
+                    nc.scalar.activation(out=level_scaled[t][:], in_=level2[t][:], func=ACT.Copy, scale=quarter_size[:, t : t + 1])
+                    nc.vector.scalar_tensor_tensor(out=groups(gap[t]), in0=groups(inv[t]), scalar=half_size[:, t : t + 1], in1=spread(level_scaled[t]), op0=ALU.mult, op1=ALU.subtract)
+                for c, half in enumerate(halves):
                     nc.scalar.activation(out=fetched[t][:, half], in_=gap[t][:].indirect(itf_sb[:, c * 16 : (c + 1) * 16]), func=ACT.Copy)
 
         def rates(planes):
             for t in planes:
-                nc.vector.tensor_tensor(out=groups(log_ratio[t]), in0=spread(log_level[t]), in1=groups(log_inv[t]), op=ALU.subtract)
-                nc.scalar.activation(out=log_ratio[t][:], in_=log_ratio[t][:], func=ACT.Relu, scale=size[:, t : t + 1])
+                if t == LAST:
+                    nc.scalar.activation(out=log_level[t][:], in_=log_level[t][:], func=ACT.Copy, scale=size[:, t : t + 1])
+                    nc.vector.scalar_tensor_tensor(out=groups(log_ratio[t]), in0=groups(log_inv[t]), scalar=minus_size[:, t : t + 1], in1=spread(log_level[t]), op0=ALU.mult, op1=ALU.add)
+                else:
+                    nc.vector.tensor_tensor(out=groups(log_ratio[t]), in0=spread(log_level[t]), in1=groups(log_inv[t]), op=ALU.subtract)
+                    nc.scalar.activation(out=log_ratio[t][:], in_=log_ratio[t][:], func=ACT.Relu, scale=size[:, t : t + 1])
 
         def combine(planes):
             for t in planes:
-                for c in range(2):
-                    half = slice(c * HALF, (c + 1) * HALF)
-                    nc.vector.scalar_tensor_tensor(out=hid[:, t, half], in0=fetched[t][:, half], scalar=0.0, in1=log_ratio[t][:, half], op0=ALU.min, op1=ALU.add)
+                for half in halves:
+                    if t == LAST:
+                        nc.vector.scalar_tensor_tensor(out=hid[:, t, half], in0=log_ratio[t][:, half], scalar=0.0, in1=fetched[t][:, half], op0=ALU.max, op1=ALU.add)
+                    else:
+                        nc.vector.scalar_tensor_tensor(out=hid[:, t, half], in0=fetched[t][:, half], scalar=0.0, in1=log_ratio[t][:, half], op0=ALU.min, op1=ALU.add)
 
         every = range(PACK)
-        logs(every)
-        exps(every)
         for t in every:
             levels([t])
             finish([t])
@@ -186,7 +206,7 @@ def tile_picked_ywater_rate_p_kernel(tc, x_words, x_scales, w1, noise, unit, w2,
             hid_bf = keep.tile([P, Q, PACK], BF16, name="hid_bf%d" % c, align_bytes=64)
             dst = hid_bf[:].rearrange("p (c i) t -> p c t i", i=4)
             src = hid[:, :, c * Q : (c + 1) * Q].rearrange("p t (c i) -> p c t i", i=4)
-            if c == 1:
+            if c % 2 == 1:
                 nc.scalar.copy(out=dst, in_=src)
             else:
                 nc.vector.tensor_copy(out=dst, in_=src)

@@ -21,7 +21,7 @@ PACK = 4
 V = S // D
 HALF = S // 2
 EXP_CAP = 1.0e13
-W1_VECTOR_SHARE = 40
+W1_VECTOR_SHARE = 96
 GAIN_FLOOR = 0.2
 
 
@@ -38,18 +38,18 @@ def tile_picked_ywater_rate_p_kernel(tc, x_words, x_scales, w1, noise, unit, w2,
         itf_sb = keep.tile([P, S // 16], U16, name="itf_sb")
         x_bytes = keep.tile([P, T], U8, name="x_bytes", align_bytes=64)
         x_codes = keep.tile([P, T], I32, name="x_codes", align_bytes=64)
-        w1_raw = [keep.tile([P, PACK, H // 2], F32, name="w1_raw%d" % c, align_bytes=64) for c in range(2)]
+        w1_raw = [keep.tile([P, PACK // 2, H], F32, name="w1_raw%d" % c, align_bytes=64) for c in range(2)]
         w2_raw = keep.tile([P, PACK, N], F32, name="w2_raw", align_bytes=64)
         unit_sb = keep.tile([P, PACK], F32, name="unit_sb")
         noise_sb = keep.tile([P, PACK, S], F32, name="noise_sb", align_bytes=64)
 
         nc.gpsimd.memset(x_bytes[:].bitcast(I32), 0)
-        nc.sync.dma_start(offs_sb[:], offs)
         w1_rows = w1.rearrange("(p j) c -> p j c", j=PACK)
-        nc.sync.dma_start(out=w1_raw[0][:], in_=w1_rows[:, :, : H // 2])
+        nc.sync.dma_start(out=w1_raw[0][:], in_=w1_rows[:, 0:2, :])
+        nc.sync.dma_start(offs_sb[:], offs)
         for q in range(4):
             nc.sync.dma_start(out=x_bytes[32 * q : 32 * q + 4, :].bitcast(I32), in_=x_scales[0, 4 * q : 4 * q + 4, :].bitcast(I32))
-        nc.sync.dma_start(out=w1_raw[1][:], in_=w1_rows[:, :, H // 2 :])
+        nc.sync.dma_start(out=w1_raw[1][:], in_=w1_rows[:, 2:4, :])
         nc.sync.dma_start(out=x_codes[:], in_=x_words[0].rearrange("p n t -> p (n t)").bitcast(I32))
         nc.sync.dma_start(itf_sb[:], itf)
         nc.sync.dma_start(out=noise_sb[:], in_=noise.rearrange("(p t) j -> p t j", t=PACK))
@@ -63,10 +63,9 @@ def tile_picked_ywater_rate_p_kernel(tc, x_words, x_scales, w1, noise, unit, w2,
         w1_bf = keep.tile([P, PACK, P, PACK], BF16, name="w1_bf", align_bytes=64)
         w1_dst = w1_bf[:].rearrange("p t m j -> p m j t")
         w1_src = [w1_raw[c][:].rearrange("p j (m t) -> p m j t", t=PACK) for c in range(2)]
-        split = P // 2 + W1_VECTOR_SHARE
-        nc.scalar.copy(out=w1_dst[:, : P // 2], in_=w1_src[0])
-        nc.vector.tensor_copy(out=w1_dst[:, P // 2 : split], in_=w1_src[1][:, :W1_VECTOR_SHARE])
-        nc.scalar.copy(out=w1_dst[:, split:], in_=w1_src[1][:, W1_VECTOR_SHARE:])
+        nc.scalar.copy(out=w1_dst[:, :, 0:2, :], in_=w1_src[0])
+        nc.vector.tensor_copy(out=w1_dst[:, :W1_VECTOR_SHARE, 2:4, :], in_=w1_src[1][:, :W1_VECTOR_SHARE])
+        nc.scalar.copy(out=w1_dst[:, W1_VECTOR_SHARE:, 2:4, :], in_=w1_src[1][:, W1_VECTOR_SHARE:])
         w1_codes = keep.tile([P, H], U32, name="w1_codes", align_bytes=64)
         w1_scales = keep.tile([P, H], U8, name="w1_scales", align_bytes=64)
         nc.vector.quantize_mx(out=w1_codes[:].bitcast(FP8X4), scales=w1_scales[:], in_=w1_bf[:].rearrange("p t m j -> p (t m j)"))
@@ -98,12 +97,13 @@ def tile_picked_ywater_rate_p_kernel(tc, x_words, x_scales, w1, noise, unit, w2,
         sign = keep.tile([P, PACK], F32, name="sign")
         half_size = keep.tile([P, PACK], F32, name="half_size")
         quarter_size = keep.tile([P, PACK], F32, name="quarter_size")
-        nc.scalar.activation(out=size[:], in_=unit_sb[:], func=ACT.Abs)
-        nc.scalar.activation(out=half_size[:], in_=unit_sb[:], func=ACT.Abs, scale=0.5)
-        nc.scalar.activation(out=quarter_size[:], in_=unit_sb[:], func=ACT.Abs, scale=0.25)
         minus_size = keep.tile([P, PACK], F32, name="minus_size")
-        nc.scalar.activation(out=minus_size[:], in_=size[:], func=ACT.Copy, scale=-1.0)
-        nc.scalar.activation(out=sign[:], in_=unit_sb[:], func=ACT.Sign)
+        nc.vector.scalar_tensor_tensor(out=size[:], in0=unit_sb[:], scalar=-1.0, in1=unit_sb[:], op0=ALU.mult, op1=ALU.max)
+        nc.vector.tensor_scalar(out=sign[:], in0=unit_sb[:], scalar1=0.0, scalar2=2.0, op0=ALU.is_ge, op1=ALU.mult)
+        nc.vector.tensor_scalar(out=half_size[:], in0=size[:], scalar1=0.5, scalar2=None, op0=ALU.mult)
+        nc.vector.tensor_scalar(out=quarter_size[:], in0=size[:], scalar1=0.25, scalar2=None, op0=ALU.mult)
+        nc.vector.tensor_scalar(out=minus_size[:], in0=size[:], scalar1=-1.0, scalar2=None, op0=ALU.mult)
+        nc.vector.tensor_scalar(out=sign[:], in0=sign[:], scalar1=-1.0, scalar2=None, op0=ALU.add)
 
         w2_bf = keep.tile([P, N, PACK], BF16, name="w2_bf", align_bytes=64)
         nc.vector.tensor_tensor(out=w2_bf[:], in0=w2_raw[:].rearrange("p j m -> p m j"),

@@ -18,24 +18,36 @@ ACT = mybir.ActivationFunctionType
 
 P = 128
 PACK = 4
-V = S // D
+GROUPS = S // D
 HALF = S // 2
+QUARTER = S // 4
+LIST_COLUMN = 16
+POWER = 2.0
+GAIN_FLOOR = 0.2
 EXP_CAP = 1.0e13
 W1_VECTOR_SHARE = 96
-GAIN_FLOOR = 0.2
+SQUARED_ON_VECTOR = (0, 1)
+CLIPPED_ON_VECTOR = (0, PACK - 1)
 
 
 def tile_picked_ywater_rate_p_kernel(tc, x_words, x_scales, w1, noise, unit, w2, offs, itf, out):
     nc = tc.nc
+    halves = [slice(0, HALF), slice(HALF, S)]
+    quarters = [slice(q * QUARTER, (q + 1) * QUARTER) for q in range(4)]
+    last_plane = PACK - 1
+
     with ExitStack() as ctx:
         keep = ctx.enter_context(tc.tile_pool(name="keep", bufs=1))
         psum = ctx.enter_context(tc.psum_pool(name="psum", bufs=1))
 
-        def rows(name, dtype=F32, width=S):
-            return [keep.tile([P, width], dtype, name="%s%d" % (name, t), align_bytes=64) for t in range(PACK)]
+        def plane_tiles(name, width=S, planes=range(PACK)):
+            return {t: keep.tile([P, width], F32, name="%s%d" % (name, t), align_bytes=64) for t in planes}
 
-        offs_sb = keep.tile([P, S // 16], U16, name="offs_sb")
-        itf_sb = keep.tile([P, S // 16], U16, name="itf_sb")
+        def entries(list_tile, cols):
+            return list_tile[:, cols.start // LIST_COLUMN : cols.stop // LIST_COLUMN]
+
+        offs_sb = keep.tile([P, S // LIST_COLUMN], U16, name="offs_sb")
+        itf_sb = keep.tile([P, S // LIST_COLUMN], U16, name="itf_sb")
         x_bytes = keep.tile([P, T], U8, name="x_bytes", align_bytes=64)
         x_codes = keep.tile([P, T], I32, name="x_codes", align_bytes=64)
         w1_raw = [keep.tile([P, PACK // 2, H], F32, name="w1_raw%d" % c, align_bytes=64) for c in range(2)]
@@ -70,26 +82,25 @@ def tile_picked_ywater_rate_p_kernel(tc, x_words, x_scales, w1, noise, unit, w2,
         w1_scales = keep.tile([P, H], U8, name="w1_scales", align_bytes=64)
         nc.vector.quantize_mx(out=w1_codes[:].bitcast(FP8X4), scales=w1_scales[:], in_=w1_bf[:].rearrange("p t m j -> p (t m j)"))
 
-        y = [psum.tile([P, S], F32, name="y%d" % t) for t in range(PACK)]
-        exp_y = rows("exp_y")
-        soft = rows("soft")
-        log_inv = rows("log_inv")
-        inv = rows("inv")
-        for c in range(2):
-            half = slice(c * HALF, (c + 1) * HALF)
-            nc.vector.tensor_copy(picked_codes[c][:], x_codes[:].bitcast(U32).indirect(offs_sb[:, c * 16 : (c + 1) * 16]))
+        y_banks = [psum.tile([P, S], F32, name="y%d" % b) for b in range(4)]
+
+        def y(t, c):
+            return y_banks[2 * c + t // 2][:, halves[t % 2]]
+
+        exp_y = plane_tiles("exp_y")
+        gain = plane_tiles("gain")
+        log_inv = plane_tiles("log_inv")
+        inv = plane_tiles("inv")
+        for c, half in enumerate(halves):
+            nc.vector.tensor_copy(picked_codes[c][:], x_codes[:].bitcast(U32).indirect(entries(offs_sb, half)))
             for t in range(PACK):
                 cols = slice(t * P, (t + 1) * P)
-                nc.tensor.matmul_mx(out=y[c * 2 + t // 2][:, (t % 2) * HALF : (t % 2 + 1) * HALF], lhsT=w1_codes[:, cols].bitcast(FP8X4), lhsT_scale=w1_scales[:, cols],
+                nc.tensor.matmul_mx(out=y(t, c), lhsT=w1_codes[:, cols].bitcast(FP8X4), lhsT_scale=w1_scales[:, cols],
                                     rhs=picked_codes[c][:].bitcast(FP8X4), rhs_scale=picked_bytes[:, half], start=True, stop=True)
 
-        def product(t, c):
-            return y[c * 2 + t // 2][:, (t % 2) * HALF : (t % 2 + 1) * HALF]
-
-        for c in range(2):
-            half = slice(c * HALF, (c + 1) * HALF)
+        for c, half in enumerate(halves):
             for t in range(PACK):
-                nc.scalar.activation(out=exp_y[t][:, half], in_=product(t, c), func=ACT.Exp)
+                nc.scalar.activation(out=exp_y[t][:, half], in_=y(t, c), func=ACT.Exp)
         for t in range(PACK):
             nc.vector.tensor_scalar(out=exp_y[t][:], in0=exp_y[t][:], scalar1=EXP_CAP, scalar2=None, op0=ALU.min)
 
@@ -112,19 +123,32 @@ def tile_picked_ywater_rate_p_kernel(tc, x_words, x_scales, w1, noise, unit, w2,
         w2_scales = keep.tile([P, N], U8, name="w2_scales", align_bytes=64)
         nc.vector.quantize_mx(out=w2_codes[:].bitcast(FP8X4), scales=w2_scales[:], in_=w2_bf[:].rearrange("p m j -> p (m j)"))
 
-        squared = exp_y
-        recip = rows("recip")
-        pair = rows("pair", width=2 * V)
-        level4 = rows("level4", width=V)
-        above4 = rows("above4")
-        pair_above = rows("pair_above", width=2 * V)
-        part = rows("part", width=V)
-        level2 = rows("level2", width=V)
-        level_scaled = rows("level_scaled", width=V)
-        log_level = rows("log_level", width=V)
-        gap = rows("gap")
-        log_ratio = rows("log_ratio")
-        fetched = rows("fetched")
+        gain_squared = exp_y
+        recip_gain = plane_tiles("recip_gain")
+        lift = math.exp(GAIN_FLOOR)
+        for t in range(PACK):
+            nc.scalar.activation(out=gain[t][:], in_=exp_y[t][:], func=ACT.Ln, scale=lift, bias=lift)
+            for c, half in enumerate(halves):
+                nc.vector.scalar_tensor_tensor(out=gain[t][:, half], in0=y(t, c), scalar=GAIN_FLOOR, in1=gain[t][:, half], op0=ALU.add, op1=ALU.max)
+                if t in SQUARED_ON_VECTOR:
+                    nc.vector.tensor_tensor(out=gain_squared[t][:, half], in0=gain[t][:, half], in1=gain[t][:, half], op=ALU.mult)
+        for t in range(PACK):
+            if t not in SQUARED_ON_VECTOR:
+                nc.scalar.activation(out=gain_squared[t][:], in_=gain[t][:], func=ACT.Square)
+            for cols in halves if t == 0 else [slice(0, S)]:
+                nc.scalar.activation(out=recip_gain[t][:, cols], in_=gain_squared[t][:, cols], func=ACT.Abs_reciprocal_sqrt)
+
+        inv_pairs = plane_tiles("inv_pairs", width=2 * GROUPS)
+        four_lvl = plane_tiles("four_lvl", width=GROUPS)
+        four_max = plane_tiles("four_max")
+        max_pairs = plane_tiles("max_pairs", width=2 * GROUPS)
+        partial = plane_tiles("partial", width=GROUPS)
+        two_final = plane_tiles("two_final", width=GROUPS)
+        sized_final = plane_tiles("sized_final", width=GROUPS, planes=[t for t in range(PACK) if t not in CLIPPED_ON_VECTOR])
+        log_final = plane_tiles("log_final", width=GROUPS)
+        power_term = plane_tiles("power_term")
+        rate_term = plane_tiles("rate_term")
+        fetched = plane_tiles("fetched")
         hid = keep.tile([P, PACK, S], F32, name="hid", align_bytes=64)
 
         def groups(tile):
@@ -134,88 +158,64 @@ def tile_picked_ywater_rate_p_kernel(tc, x_words, x_scales, w1, noise, unit, w2,
             return tile[:].rearrange("p (v e) -> p v e", e=2)
 
         def spread(tile):
-            return tile[:].unsqueeze(2).to_broadcast([P, V, D])
+            return tile[:].unsqueeze(2).to_broadcast([P, GROUPS, D])
 
-        halves = [slice(c * HALF, (c + 1) * HALF) for c in range(2)]
-        lift = math.exp(GAIN_FLOOR)
         for t in range(PACK):
-            nc.scalar.activation(out=soft[t][:], in_=exp_y[t][:], func=ACT.Ln, scale=lift, bias=lift)
-            for c, half in enumerate(halves):
-                nc.vector.scalar_tensor_tensor(out=soft[t][:, half], in0=product(t, c), scalar=GAIN_FLOOR, in1=soft[t][:, half], op0=ALU.add, op1=ALU.max)
-                if t < 2:
-                    nc.vector.tensor_tensor(out=squared[t][:, half], in0=soft[t][:, half], in1=soft[t][:, half], op=ALU.mult)
-        for half in halves:
-            nc.scalar.activation(out=recip[0][:, half], in_=squared[0][:, half], func=ACT.Abs_reciprocal_sqrt)
-        for t in range(1, PACK):
-            if t >= 2:
-                nc.scalar.activation(out=squared[t][:], in_=soft[t][:], func=ACT.Square)
-            nc.scalar.activation(out=recip[t][:], in_=squared[t][:], func=ACT.Abs_reciprocal_sqrt)
-        for t in range(PACK):
-            nc.vector.tensor_tensor(out=inv[t][:], in0=recip[t][:], in1=noise_sb[:, t, :], op=ALU.mult)
-            nc.scalar.activation(out=log_inv[t][:], in_=inv[t][:], func=ACT.Ln)
+            column = slice(t, t + 1)
+            nc.vector.tensor_tensor(out=inv[t][:], in0=recip_gain[t][:], in1=noise_sb[:, t, :], op=ALU.mult)
+            nc.vector.tensor_tensor(out=pairs(inv_pairs[t]), in0=groups(inv[t])[:, :, 0:2], in1=groups(inv[t])[:, :, 2:4], op=ALU.add)
+            nc.vector.scalar_tensor_tensor(out=four_lvl[t][:], in0=pairs(inv_pairs[t])[:, :, 0], scalar=POWER, in1=pairs(inv_pairs[t])[:, :, 1], op0=ALU.add, op1=ALU.add)
+            nc.vector.scalar_tensor_tensor(out=groups(four_max[t]), in0=groups(inv[t]), scalar=4.0, in1=spread(four_lvl[t]), op0=ALU.mult, op1=ALU.max)
+            nc.vector.tensor_tensor(out=pairs(max_pairs[t]), in0=groups(four_max[t])[:, :, 0:2], in1=groups(four_max[t])[:, :, 2:4], op=ALU.add)
+            nc.vector.scalar_tensor_tensor(out=partial[t][:], in0=pairs(max_pairs[t])[:, :, 0], scalar=-0.125, in1=four_lvl[t][:], op0=ALU.mult, op1=ALU.add)
+            nc.vector.scalar_tensor_tensor(out=two_final[t][:], in0=pairs(max_pairs[t])[:, :, 1], scalar=-0.125, in1=partial[t][:], op0=ALU.mult, op1=ALU.add)
+            nc.scalar.activation(out=log_final[t][:], in_=two_final[t][:], func=ACT.Ln, scale=0.5)
 
-        def levels(planes):
-            for t in planes:
-                nc.vector.tensor_tensor(out=pairs(pair[t]), in0=groups(inv[t])[:, :, 0:2], in1=groups(inv[t])[:, :, 2:4], op=ALU.add)
-                nc.vector.scalar_tensor_tensor(out=level4[t][:], in0=pairs(pair[t])[:, :, 0], scalar=2.0, in1=pairs(pair[t])[:, :, 1], op0=ALU.add, op1=ALU.add)
-                nc.vector.scalar_tensor_tensor(out=groups(above4[t]), in0=groups(inv[t]), scalar=4.0, in1=spread(level4[t]), op0=ALU.mult, op1=ALU.max)
-                nc.vector.tensor_tensor(out=pairs(pair_above[t]), in0=groups(above4[t])[:, :, 0:2], in1=groups(above4[t])[:, :, 2:4], op=ALU.add)
-                nc.vector.scalar_tensor_tensor(out=part[t][:], in0=pairs(pair_above[t])[:, :, 0], scalar=-0.125, in1=level4[t][:], op0=ALU.mult, op1=ALU.add)
-                nc.vector.scalar_tensor_tensor(out=level2[t][:], in0=pairs(pair_above[t])[:, :, 1], scalar=-0.125, in1=part[t][:], op0=ALU.mult, op1=ALU.add)
-                nc.scalar.activation(out=log_level[t][:], in_=level2[t][:], func=ACT.Ln, scale=0.5)
-
-        LAST = PACK - 1
-
-        def finish(planes):
-            for t in planes:
-                if t == LAST:
-                    nc.vector.scalar_tensor_tensor(out=groups(gap[t]), in0=groups(inv[t]), scalar=2.0, in1=spread(level2[t]), op0=ALU.mult, op1=ALU.subtract)
-                    nc.vector.tensor_scalar(out=gap[t][:], in0=gap[t][:], scalar1=0.0, scalar2=quarter_size[:, t : t + 1], op0=ALU.min, op1=ALU.mult)
-                else:
-                    nc.scalar.activation(out=level_scaled[t][:], in_=level2[t][:], func=ACT.Copy, scale=quarter_size[:, t : t + 1])
-                    nc.vector.scalar_tensor_tensor(out=groups(gap[t]), in0=groups(inv[t]), scalar=half_size[:, t : t + 1], in1=spread(level_scaled[t]), op0=ALU.mult, op1=ALU.subtract)
-                for c, half in enumerate(halves):
-                    nc.scalar.activation(out=fetched[t][:, half], in_=gap[t][:].indirect(itf_sb[:, c * 16 : (c + 1) * 16]), func=ACT.Copy)
-
-        def rates(planes):
-            for t in planes:
-                if t == LAST:
-                    nc.scalar.activation(out=log_level[t][:], in_=log_level[t][:], func=ACT.Copy, scale=size[:, t : t + 1])
-                    nc.vector.scalar_tensor_tensor(out=groups(log_ratio[t]), in0=groups(log_inv[t]), scalar=minus_size[:, t : t + 1], in1=spread(log_level[t]), op0=ALU.mult, op1=ALU.add)
-                else:
-                    nc.vector.tensor_tensor(out=groups(log_ratio[t]), in0=spread(log_level[t]), in1=groups(log_inv[t]), op=ALU.subtract)
-                    nc.scalar.activation(out=log_ratio[t][:], in_=log_ratio[t][:], func=ACT.Relu, scale=size[:, t : t + 1])
-
-        def combine(planes):
-            for t in planes:
-                for half in halves:
-                    if t == LAST:
-                        nc.vector.scalar_tensor_tensor(out=hid[:, t, half], in0=log_ratio[t][:, half], scalar=0.0, in1=fetched[t][:, half], op0=ALU.max, op1=ALU.add)
-                    else:
-                        nc.vector.scalar_tensor_tensor(out=hid[:, t, half], in0=fetched[t][:, half], scalar=0.0, in1=log_ratio[t][:, half], op0=ALU.min, op1=ALU.add)
-
-        every = range(PACK)
-        for t in every:
-            levels([t])
-            finish([t])
-        rates(every)
-        combine(every)
-
-        Q = 128
-        for c in range(S // Q):
-            hid_bf = keep.tile([P, Q, PACK], BF16, name="hid_bf%d" % c, align_bytes=64)
-            dst = hid_bf[:].rearrange("p (c i) t -> p c t i", i=4)
-            src = hid[:, :, c * Q : (c + 1) * Q].rearrange("p t (c i) -> p c t i", i=4)
-            if c % 2 == 1:
-                nc.scalar.copy(out=dst, in_=src)
+            if t in CLIPPED_ON_VECTOR:
+                nc.vector.scalar_tensor_tensor(out=groups(power_term[t]), in0=groups(inv[t]), scalar=2.0, in1=spread(two_final[t]), op0=ALU.mult, op1=ALU.subtract)
+                nc.vector.tensor_scalar(out=power_term[t][:], in0=power_term[t][:], scalar1=0.0, scalar2=quarter_size[:, column], op0=ALU.min, op1=ALU.mult)
             else:
-                nc.vector.tensor_copy(out=dst, in_=src)
-            hid_codes = keep.tile([P, Q], U32, name="hid_codes%d" % c, align_bytes=64)
-            hid_scales = keep.tile([P, Q], U8, name="hid_scales%d" % c, align_bytes=64)
+                nc.scalar.activation(out=sized_final[t][:], in_=two_final[t][:], func=ACT.Copy, scale=quarter_size[:, column])
+                nc.vector.scalar_tensor_tensor(out=groups(power_term[t]), in0=groups(inv[t]), scalar=half_size[:, column], in1=spread(sized_final[t]), op0=ALU.mult, op1=ALU.subtract)
+            for cols in [halves[0]] + quarters[2:] if t == last_plane else halves:
+                nc.scalar.activation(out=fetched[t][:, cols], in_=power_term[t][:].indirect(entries(itf_sb, cols)), func=ACT.Copy)
+
+        for t in range(PACK):
+            column = slice(t, t + 1)
+            nc.scalar.activation(out=log_inv[t][:], in_=inv[t][:], func=ACT.Ln)
+            if t in CLIPPED_ON_VECTOR:
+                nc.scalar.activation(out=log_final[t][:], in_=log_final[t][:], func=ACT.Copy, scale=size[:, column])
+                nc.vector.scalar_tensor_tensor(out=groups(rate_term[t]), in0=groups(log_inv[t]), scalar=minus_size[:, column], in1=spread(log_final[t]), op0=ALU.mult, op1=ALU.add)
+            else:
+                nc.vector.tensor_tensor(out=groups(rate_term[t]), in0=spread(log_final[t]), in1=groups(log_inv[t]), op=ALU.subtract)
+                nc.scalar.activation(out=rate_term[t][:], in_=rate_term[t][:], func=ACT.Relu, scale=size[:, column])
+
+        def make_hid(t, cols):
+            if t in CLIPPED_ON_VECTOR:
+                nc.vector.scalar_tensor_tensor(out=hid[:, t, cols], in0=rate_term[t][:, cols], scalar=0.0, in1=fetched[t][:, cols], op0=ALU.max, op1=ALU.add)
+            else:
+                nc.vector.scalar_tensor_tensor(out=hid[:, t, cols], in0=fetched[t][:, cols], scalar=0.0, in1=rate_term[t][:, cols], op0=ALU.min, op1=ALU.add)
+
+        def second_product(q, interleave, empty_bank):
+            hid_bf = keep.tile([P, QUARTER, PACK], BF16, name="hid_bf%d" % q, align_bytes=64)
+            interleave(out=hid_bf[:].rearrange("p (c i) t -> p c t i", i=4), in_=hid[:, :, quarters[q]].rearrange("p t (c i) -> p c t i", i=4))
+            hid_codes = keep.tile([P, QUARTER], U32, name="hid_codes%d" % q, align_bytes=64)
+            hid_scales = keep.tile([P, QUARTER], U8, name="hid_scales%d" % q, align_bytes=64)
             nc.vector.quantize_mx(out=hid_codes[:].bitcast(FP8X4), scales=hid_scales[:], in_=hid_bf[:].rearrange("p j t -> p (j t)"))
-            acc = psum.tile([P, Q], F32, name="acc%d" % c)
+            acc = psum.tile([P, QUARTER], F32, name="acc%d" % q)
             nc.tensor.matmul_mx(out=acc[:], lhsT=w2_codes[:].bitcast(FP8X4), lhsT_scale=w2_scales[:],
                                 rhs=hid_codes[:].bitcast(FP8X4), rhs_scale=hid_scales[:], start=True, stop=True)
-            res = keep.tile([P, Q], F32, name="res%d" % c, align_bytes=64)
-            nc.scalar.copy(out=res[:], in_=acc[:])
-            nc.sync.dma_start(out=out[:, c * Q : (c + 1) * Q], in_=res[:])
+            result = keep.tile([P, QUARTER], F32, name="result%d" % q, align_bytes=64)
+            empty_bank(out=result[:], in_=acc[:])
+            nc.sync.dma_start(out=out[:, quarters[q]], in_=result[:])
+
+        for t in range(PACK):
+            make_hid(t, halves[0])
+        second_product(0, nc.scalar.copy, nc.scalar.copy)
+        second_product(1, nc.scalar.copy, nc.scalar.copy)
+        for t in range(last_plane):
+            make_hid(t, halves[1])
+        make_hid(last_plane, quarters[2])
+        second_product(2, nc.vector.tensor_copy, nc.vector.tensor_copy)
+        make_hid(last_plane, quarters[3])
+        second_product(3, nc.vector.tensor_copy, nc.scalar.copy)

import math
from contextlib import ExitStack

import concourse.mybir as mybir

K, T, S, D, N, H = 512, 2048, 512, 4, 128, 512
FLOPS = 2 * K * H * S + 2 * H * N * S

F32 = mybir.dt.float32
BF16 = mybir.dt.bfloat16
I32 = mybir.dt.int32
U32 = mybir.dt.uint32
U16 = mybir.dt.uint16
U8 = mybir.dt.uint8
FP8X4 = mybir.dt.float8_e4m3fn_x4
ALU = mybir.AluOpType
ACT = mybir.ActivationFunctionType

P = 128
PACK = 4
GROUPS = S // D
HALF = S // 2
QUARTER = S // 4
LIST_COLUMN = 16
POWER = 2.0
GAIN_FLOOR = 0.2
EXP_CAP = 1.0e13
W1_VECTOR_SHARE = 96
SQUARED_ON_VECTOR = (0, 1)
CLIPPED_ON_VECTOR = (0, PACK - 1)


def tile_picked_ywater_rate_p_kernel(tc, x_words, x_scales, w1, noise, unit, w2, offs, itf, out):
    nc = tc.nc
    halves = [slice(0, HALF), slice(HALF, S)]
    quarters = [slice(q * QUARTER, (q + 1) * QUARTER) for q in range(4)]
    last_plane = PACK - 1

    with ExitStack() as ctx:
        keep = ctx.enter_context(tc.tile_pool(name="keep", bufs=1))
        psum = ctx.enter_context(tc.psum_pool(name="psum", bufs=1))

        def plane_tiles(name, width=S, planes=range(PACK)):
            return {t: keep.tile([P, width], F32, name="%s%d" % (name, t), align_bytes=64) for t in planes}

        def entries(list_tile, cols):
            return list_tile[:, cols.start // LIST_COLUMN : cols.stop // LIST_COLUMN]

        offs_sb = keep.tile([P, S // LIST_COLUMN], U16, name="offs_sb")
        itf_sb = keep.tile([P, S // LIST_COLUMN], U16, name="itf_sb")
        x_bytes = keep.tile([P, T], U8, name="x_bytes", align_bytes=64)
        x_codes = keep.tile([P, T], I32, name="x_codes", align_bytes=64)
        w1_raw = [keep.tile([P, PACK // 2, H], F32, name="w1_raw%d" % c, align_bytes=64) for c in range(2)]
        w2_raw = keep.tile([P, PACK, N], F32, name="w2_raw", align_bytes=64)
        unit_sb = keep.tile([P, PACK], F32, name="unit_sb")
        noise_sb = keep.tile([P, PACK, S], F32, name="noise_sb", align_bytes=64)

        nc.gpsimd.memset(x_bytes[:].bitcast(I32), 0)
        w1_rows = w1.rearrange("(p j) c -> p j c", j=PACK)
        nc.sync.dma_start(out=w1_raw[0][:], in_=w1_rows[:, 0:2, :])
        nc.sync.dma_start(offs_sb[:], offs)
        for q in range(4):
            nc.sync.dma_start(out=x_bytes[32 * q : 32 * q + 4, :].bitcast(I32), in_=x_scales[0, 4 * q : 4 * q + 4, :].bitcast(I32))
        nc.sync.dma_start(out=w1_raw[1][:], in_=w1_rows[:, 2:4, :])
        nc.sync.dma_start(out=x_codes[:], in_=x_words[0].rearrange("p n t -> p (n t)").bitcast(I32))
        nc.sync.dma_start(itf_sb[:], itf)
        nc.sync.dma_start(out=noise_sb[:], in_=noise.rearrange("(p t) j -> p t j", t=PACK))
        nc.sync.dma_start(out=unit_sb[:], in_=unit.rearrange("(p t) o -> p (t o)", t=PACK))
        nc.sync.dma_start(out=w2_raw[:], in_=w2.rearrange("(p j) m -> p j m", j=PACK))

        picked_bytes = keep.tile([P, S], U8, name="picked_bytes", align_bytes=64)
        picked_codes = [keep.tile([P, HALF], U32, name="picked_codes%d" % c, align_bytes=64) for c in range(2)]
        nc.vector.tensor_copy(picked_bytes[:], x_bytes[:].indirect(offs_sb[:]))

        w1_bf = keep.tile([P, PACK, P, PACK], BF16, name="w1_bf", align_bytes=64)
        w1_dst = w1_bf[:].rearrange("p t m j -> p m j t")
        w1_src = [w1_raw[c][:].rearrange("p j (m t) -> p m j t", t=PACK) for c in range(2)]
        nc.scalar.copy(out=w1_dst[:, :, 0:2, :], in_=w1_src[0])
        nc.vector.tensor_copy(out=w1_dst[:, :W1_VECTOR_SHARE, 2:4, :], in_=w1_src[1][:, :W1_VECTOR_SHARE])
        nc.scalar.copy(out=w1_dst[:, W1_VECTOR_SHARE:, 2:4, :], in_=w1_src[1][:, W1_VECTOR_SHARE:])
        w1_codes = keep.tile([P, H], U32, name="w1_codes", align_bytes=64)
        w1_scales = keep.tile([P, H], U8, name="w1_scales", align_bytes=64)
        nc.vector.quantize_mx(out=w1_codes[:].bitcast(FP8X4), scales=w1_scales[:], in_=w1_bf[:].rearrange("p t m j -> p (t m j)"))

        y_banks = [psum.tile([P, S], F32, name="y%d" % b) for b in range(4)]

        def y(t, c):
            return y_banks[2 * c + t // 2][:, halves[t % 2]]

        exp_y = plane_tiles("exp_y")
        gain = plane_tiles("gain")
        log_inv = plane_tiles("log_inv")
        inv = plane_tiles("inv")
        for c, half in enumerate(halves):
            nc.vector.tensor_copy(picked_codes[c][:], x_codes[:].bitcast(U32).indirect(entries(offs_sb, half)))
            for t in range(PACK):
                cols = slice(t * P, (t + 1) * P)
                nc.tensor.matmul_mx(out=y(t, c), lhsT=w1_codes[:, cols].bitcast(FP8X4), lhsT_scale=w1_scales[:, cols],
                                    rhs=picked_codes[c][:].bitcast(FP8X4), rhs_scale=picked_bytes[:, half], start=True, stop=True)

        for c, half in enumerate(halves):
            for t in range(PACK):
                nc.scalar.activation(out=exp_y[t][:, half], in_=y(t, c), func=ACT.Exp)
        for t in range(PACK):
            nc.vector.tensor_scalar(out=exp_y[t][:], in0=exp_y[t][:], scalar1=EXP_CAP, scalar2=None, op0=ALU.min)

        size = keep.tile([P, PACK], F32, name="size")
        sign = keep.tile([P, PACK], F32, name="sign")
        half_size = keep.tile([P, PACK], F32, name="half_size")
        quarter_size = keep.tile([P, PACK], F32, name="quarter_size")
        minus_size = keep.tile([P, PACK], F32, name="minus_size")
        nc.vector.scalar_tensor_tensor(out=size[:], in0=unit_sb[:], scalar=-1.0, in1=unit_sb[:], op0=ALU.mult, op1=ALU.max)
        nc.vector.tensor_scalar(out=sign[:], in0=unit_sb[:], scalar1=0.0, scalar2=2.0, op0=ALU.is_ge, op1=ALU.mult)
        nc.vector.tensor_scalar(out=half_size[:], in0=size[:], scalar1=0.5, scalar2=None, op0=ALU.mult)
        nc.vector.tensor_scalar(out=quarter_size[:], in0=size[:], scalar1=0.25, scalar2=None, op0=ALU.mult)
        nc.vector.tensor_scalar(out=minus_size[:], in0=size[:], scalar1=-1.0, scalar2=None, op0=ALU.mult)
        nc.vector.tensor_scalar(out=sign[:], in0=sign[:], scalar1=-1.0, scalar2=None, op0=ALU.add)

        w2_bf = keep.tile([P, N, PACK], BF16, name="w2_bf", align_bytes=64)
        nc.vector.tensor_tensor(out=w2_bf[:], in0=w2_raw[:].rearrange("p j m -> p m j"),
                                in1=sign[:].unsqueeze(1).to_broadcast([P, N, PACK]), op=ALU.mult)
        w2_codes = keep.tile([P, N], U32, name="w2_codes", align_bytes=64)
        w2_scales = keep.tile([P, N], U8, name="w2_scales", align_bytes=64)
        nc.vector.quantize_mx(out=w2_codes[:].bitcast(FP8X4), scales=w2_scales[:], in_=w2_bf[:].rearrange("p m j -> p (m j)"))

        gain_squared = exp_y
        recip_gain = plane_tiles("recip_gain")
        lift = math.exp(GAIN_FLOOR)
        for t in range(PACK):
            nc.scalar.activation(out=gain[t][:], in_=exp_y[t][:], func=ACT.Ln, scale=lift, bias=lift)
            for c, half in enumerate(halves):
                nc.vector.scalar_tensor_tensor(out=gain[t][:, half], in0=y(t, c), scalar=GAIN_FLOOR, in1=gain[t][:, half], op0=ALU.add, op1=ALU.max)
                if t in SQUARED_ON_VECTOR:
                    nc.vector.tensor_tensor(out=gain_squared[t][:, half], in0=gain[t][:, half], in1=gain[t][:, half], op=ALU.mult)
        for t in range(PACK):
            if t not in SQUARED_ON_VECTOR:
                nc.scalar.activation(out=gain_squared[t][:], in_=gain[t][:], func=ACT.Square)
            for cols in halves if t == 0 else [slice(0, S)]:
                nc.scalar.activation(out=recip_gain[t][:, cols], in_=gain_squared[t][:, cols], func=ACT.Abs_reciprocal_sqrt)

        inv_pairs = plane_tiles("inv_pairs", width=2 * GROUPS)
        four_lvl = plane_tiles("four_lvl", width=GROUPS)
        four_max = plane_tiles("four_max")
        max_pairs = plane_tiles("max_pairs", width=2 * GROUPS)
        partial = plane_tiles("partial", width=GROUPS)
        two_final = plane_tiles("two_final", width=GROUPS)
        sized_final = plane_tiles("sized_final", width=GROUPS, planes=[t for t in range(PACK) if t not in CLIPPED_ON_VECTOR])
        log_final = plane_tiles("log_final", width=GROUPS)
        power_term = plane_tiles("power_term")
        rate_term = plane_tiles("rate_term")
        fetched = plane_tiles("fetched")
        hid = keep.tile([P, PACK, S], F32, name="hid", align_bytes=64)

        def groups(tile):
            return tile[:].rearrange("p (v d) -> p v d", d=D)

        def pairs(tile):
            return tile[:].rearrange("p (v e) -> p v e", e=2)

        def spread(tile):
            return tile[:].unsqueeze(2).to_broadcast([P, GROUPS, D])

        for t in range(PACK):
            column = slice(t, t + 1)
            nc.vector.tensor_tensor(out=inv[t][:], in0=recip_gain[t][:], in1=noise_sb[:, t, :], op=ALU.mult)
            nc.vector.tensor_tensor(out=pairs(inv_pairs[t]), in0=groups(inv[t])[:, :, 0:2], in1=groups(inv[t])[:, :, 2:4], op=ALU.add)
            nc.vector.scalar_tensor_tensor(out=four_lvl[t][:], in0=pairs(inv_pairs[t])[:, :, 0], scalar=POWER, in1=pairs(inv_pairs[t])[:, :, 1], op0=ALU.add, op1=ALU.add)
            nc.vector.scalar_tensor_tensor(out=groups(four_max[t]), in0=groups(inv[t]), scalar=4.0, in1=spread(four_lvl[t]), op0=ALU.mult, op1=ALU.max)
            nc.vector.tensor_tensor(out=pairs(max_pairs[t]), in0=groups(four_max[t])[:, :, 0:2], in1=groups(four_max[t])[:, :, 2:4], op=ALU.add)
            nc.vector.scalar_tensor_tensor(out=partial[t][:], in0=pairs(max_pairs[t])[:, :, 0], scalar=-0.125, in1=four_lvl[t][:], op0=ALU.mult, op1=ALU.add)
            nc.vector.scalar_tensor_tensor(out=two_final[t][:], in0=pairs(max_pairs[t])[:, :, 1], scalar=-0.125, in1=partial[t][:], op0=ALU.mult, op1=ALU.add)
            nc.scalar.activation(out=log_final[t][:], in_=two_final[t][:], func=ACT.Ln, scale=0.5)

            if t in CLIPPED_ON_VECTOR:
                nc.vector.scalar_tensor_tensor(out=groups(power_term[t]), in0=groups(inv[t]), scalar=2.0, in1=spread(two_final[t]), op0=ALU.mult, op1=ALU.subtract)
                nc.vector.tensor_scalar(out=power_term[t][:], in0=power_term[t][:], scalar1=0.0, scalar2=quarter_size[:, column], op0=ALU.min, op1=ALU.mult)
            else:
                nc.scalar.activation(out=sized_final[t][:], in_=two_final[t][:], func=ACT.Copy, scale=quarter_size[:, column])
                nc.vector.scalar_tensor_tensor(out=groups(power_term[t]), in0=groups(inv[t]), scalar=half_size[:, column], in1=spread(sized_final[t]), op0=ALU.mult, op1=ALU.subtract)
            for cols in [halves[0]] + quarters[2:] if t == last_plane else halves:
                nc.scalar.activation(out=fetched[t][:, cols], in_=power_term[t][:].indirect(entries(itf_sb, cols)), func=ACT.Copy)

        for t in range(PACK):
            column = slice(t, t + 1)
            nc.scalar.activation(out=log_inv[t][:], in_=inv[t][:], func=ACT.Ln)
            if t in CLIPPED_ON_VECTOR:
                nc.scalar.activation(out=log_final[t][:], in_=log_final[t][:], func=ACT.Copy, scale=size[:, column])
                nc.vector.scalar_tensor_tensor(out=groups(rate_term[t]), in0=groups(log_inv[t]), scalar=minus_size[:, column], in1=spread(log_final[t]), op0=ALU.mult, op1=ALU.add)
            else:
                nc.vector.tensor_tensor(out=groups(rate_term[t]), in0=spread(log_final[t]), in1=groups(log_inv[t]), op=ALU.subtract)
                nc.scalar.activation(out=rate_term[t][:], in_=rate_term[t][:], func=ACT.Relu, scale=size[:, column])

        def make_hid(t, cols):
            if t in CLIPPED_ON_VECTOR:
                nc.vector.scalar_tensor_tensor(out=hid[:, t, cols], in0=rate_term[t][:, cols], scalar=0.0, in1=fetched[t][:, cols], op0=ALU.max, op1=ALU.add)
            else:
                nc.vector.scalar_tensor_tensor(out=hid[:, t, cols], in0=fetched[t][:, cols], scalar=0.0, in1=rate_term[t][:, cols], op0=ALU.min, op1=ALU.add)

        def second_product(q, interleave, empty_bank):
            hid_bf = keep.tile([P, QUARTER, PACK], BF16, name="hid_bf%d" % q, align_bytes=64)
            interleave(out=hid_bf[:].rearrange("p (c i) t -> p c t i", i=4), in_=hid[:, :, quarters[q]].rearrange("p t (c i) -> p c t i", i=4))
            hid_codes = keep.tile([P, QUARTER], U32, name="hid_codes%d" % q, align_bytes=64)
            hid_scales = keep.tile([P, QUARTER], U8, name="hid_scales%d" % q, align_bytes=64)
            nc.vector.quantize_mx(out=hid_codes[:].bitcast(FP8X4), scales=hid_scales[:], in_=hid_bf[:].rearrange("p j t -> p (j t)"))
            acc = psum.tile([P, QUARTER], F32, name="acc%d" % q)
            nc.tensor.matmul_mx(out=acc[:], lhsT=w2_codes[:].bitcast(FP8X4), lhsT_scale=w2_scales[:],
                                rhs=hid_codes[:].bitcast(FP8X4), rhs_scale=hid_scales[:], start=True, stop=True)
            result = keep.tile([P, QUARTER], F32, name="result%d" % q, align_bytes=64)
            empty_bank(out=result[:], in_=acc[:])
            nc.sync.dma_start(out=out[:, quarters[q]], in_=result[:])

        for t in range(PACK):
            make_hid(t, halves[0])
        second_product(0, nc.scalar.copy, nc.scalar.copy)
        second_product(1, nc.scalar.copy, nc.scalar.copy)
        for t in range(last_plane):
            make_hid(t, halves[1])
        make_hid(last_plane, quarters[2])
        second_product(2, nc.vector.tensor_copy, nc.vector.tensor_copy)
        make_hid(last_plane, quarters[3])
        second_product(3, nc.vector.tensor_copy, nc.scalar.copy)
